import numpy as np, ml_dtypes
CORES = [100,101,102,103,108,109,110,111]
N = 8
import mx_ref
KO = 3
F = np.float32(0.8)
OWN = [7,7,7,7,7,7,7,7]
BF = ml_dtypes.bfloat16
def tile(rs):
    return np.stack(rs, axis=2).reshape(128, -1).astype(BF)
def pick(b):
    s = np.zeros((128, 128, 4), np.float32)
    s[np.arange(128), np.arange(128), b] = 1.0
    return mx_ref.quantize(s.reshape(128, 512).astype(BF))
def pk(c, s, i=0):
    return (np.ascontiguousarray(c[:, 512 * i:512 * i + 512]), mx_ref.live(s[:, 128 * i:128 * i + 128]))
def inputs(rng, e, E):
    def f(*shape):
        v = (rng.standard_normal(shape, dtype=np.float32) * np.exp2(rng.integers(-2, 3, shape[:-1] + (1,)))).astype(BF)
        return mx_ref.spread((v.astype(np.float32) * np.exp2(rng.integers(-E, E + 1, shape[:-2] + (1, 1))).astype(np.float32)).astype(BF), rng, e)
    def packed(k):
        c = np.zeros((N, 128, k * 512), np.uint8); s = np.zeros((N, 128, k * 128), np.uint8)
        for r in range(N):
            for i in range(k):
                a, b = mx_ref.quantize(f(128, 512)); c[r][:, 512 * i:512 * i + 512] = a; s[r][:, 128 * i:128 * i + 128] = mx_ref.plane(b, rng)
        return c, s
    d = {}
    d["kc"], d["ks"] = packed(KO)
    d["q"] = f(N, 128, 512)
    return d
def setup_inputs(rng):
    return inputs(rng, 0, 0)
def setup_inputs_blocks(rng):
    return inputs(rng, 4, 0)
def setup_inputs_wide(rng):
    return inputs(rng, 0, 8)
def reference(kc, ks, q):
    S = [pick(t) for t in range(4)]
    anew = lambda p, i: mx_ref.quantize(tile([mx_ref.matmul(S[t], pk(kc[p], ks[p], i)) * F for t in range(4)]))
    y = np.full((N, 128, 3072), np.nan, np.float32)
    for o in range(N):
        if OWN[o] != o: continue
        qq = mx_ref.quantize(q[o])
        M = [pk(kc[o], ks[o], i) for i in range(KO)] + [anew(p, i) for p in range(N) if p != o and OWN[p] == o for i in range(KO)]
        y[o][:, :128 * len(M)] = np.concatenate([mx_ref.matmul(qq, m) for m in M], axis=1)
    return {"y": y}

@@ -1,0 +1,192 @@
+from concourse.mybir import dt, AluOpType, ActivationFunctionType
+
+KT = 384
+NR = 8
+BANK = 512
+NBANK = 8
+MAXP = 3
+SCALE = 0.8
+
+SCRATCH = {
+    "kcb": ("sbuf", [128, KT], "float8_e4m3fn_x4"),
+    "ksb": ("sbuf", [128, KT], "uint8"),
+    "z": ("sbuf", [128, 516], "bfloat16"),
+    "sc": ("sbuf", [128, 512], "float8_e4m3fn_x4"),
+    "ss": ("sbuf", [128, 512], "uint8"),
+    "t": ("sbuf", [128, 4 * KT], "bfloat16"),
+    "nc": ("sbuf", [128, KT], "float8_e4m3fn_x4"),
+    "ns": ("sbuf", [128, KT], "uint8"),
+    "qb": ("sbuf", [128, 512], "bfloat16"),
+    "qc": ("sbuf", [128, 128], "float8_e4m3fn_x4"),
+    "qs": ("sbuf", [128, 128], "uint8"),
+    "lc": ("sbuf", [128, NR * KT], "float8_e4m3fn_x4"),
+    "ls": ("sbuf", [128, NR * KT], "uint8"),
+    "yb": ("sbuf", [128, NR * KT], "float32"),
+    "ps": ("psum", [128, BANK * NBANK], "float32"),
+}
+SEMAPHORES = (["ldq", "lds", "zero", "one", "qq", "sent", "store", "store2"]
+              + ["ldc%d" % k for k in range(MAXP)]
+              + ["sel%d" % b for b in range(4)]
+              + ["mm%d_%d" % (k, b) for k in range(MAXP) for b in range(4)]
+              + ["ev%d_%d" % (k, b) for k in range(MAXP) for b in range(4)]
+              + ["new%d" % k for k in range(MAXP)]
+              + ["arr%d_%d" % (r, k) for r in range(NR) for k in range(MAXP)]
+              + ["um%d" % u for u in range(NR * MAXP)]
+              + ["ue%d" % u for u in range(NR * MAXP)])
+
+
+def engines(topo, src, dst):
+    m = topo.mask(src, dst)
+    bits = [i for i in range(m.bit_length()) if (m >> i) & 1]
+    if topo.chip(src) == topo.chip(dst):
+        bits = bits[::2]
+    return sum(1 << i for i in bits), len(bits)
+
+
+def plan(T, topo):
+    own = T.tables["OWN"]
+    out = {}
+    blocked = 0
+    for r, c in enumerate(T.cores):
+        if own[r] == r:
+            continue
+        dst = T.cores[own[r]]
+        if topo.may_write(c, dst):
+            cols, via = [(0, KT)], None
+        else:
+            idle = [x for x in range(8 * topo.chip(c), 8 * topo.chip(c) + 8)
+                    if x not in T.cores and topo.chip(x) == topo.chip(c) and topo.may_write(x, dst)]
+            via = idle[blocked % len(idle)]
+            blocked += 1
+            cols = [(0, KT // 2), (KT // 2, KT // 2)]
+        out[r] = [(a, n, via) for a, n in cols]
+    return out
+
+
+def send(g, T, topo, src, dst, codes, scales, r, a, n, sem):
+    mask, ne = engines(topo, src, dst)
+    rid, pid, _s = topo.addr(dst)
+    lo = r * KT + a
+    g.remote_dma(T.lc[:, lo:lo + n].bitcast(dt.uint8), codes.bitcast(dt.uint8), sem, T.sem["sent"], pid, rid, mask)
+    g.remote_dma(T.ls[:, lo:lo + n], scales, sem, T.sem["sent"], pid, rid, mask)
+    return 2 * ne
+
+
+def forward(g, core, T, topo, routes, own):
+    sent = 0
+    todo = [(k, r, p) for r in routes for k, p in enumerate(routes[r]) if p[2] == core]
+    for k, r, (a, n, _via) in sorted(todo):
+        _m, ne = engines(topo, T.cores[r], core)
+        sem = T.sem["arr%d_%d" % (r, k)]
+        lo = r * KT + a
+        g.wait_ge(sem, 2 * ne)
+        sent += send(g, T, topo, core, T.cores[own[r]], T.lc[:, lo:lo + n], T.ls[:, lo:lo + n], r, a, n, sem)
+    return sent
+
+
+def producer(g, core, T, topo, routes, own, r):
+    pieces = routes[r]
+    for k, (a, n, _v) in enumerate(pieces):
+        g.sync.dma_start(T.kcb[:, a:a + n].bitcast(dt.uint8), T.kc[:, 4 * a:4 * (a + n)]).then_inc(T.sem["ldc%d" % k], 16)
+    g.scalar.dma_start(T.ksb[:], T.ks[:]).then_inc(T.sem["lds"], 16)
+    g.vector.memset(T.z[:], 0.0).then_inc(T.sem["zero"], 1)
+    g.wait_ge(T.sem["zero"], 1)
+    g.affine_select(T.z[:, 3:515:4], T.z[:, 3:515:4], [[-1, 128]], AluOpType.not_equal, 1.0, 0, 1).then_inc(T.sem["one"], 1)
+    g.vector.wait_ge(T.sem["one"], 1)
+    for b in range(4):
+        g.vector.quantize_mx(T.sc[:, 128 * b:128 * b + 128], T.ss[:, 128 * b:128 * b + 128],
+                             T.z[:, 3 - b:515 - b]).then_inc(T.sem["sel%d" % b], 1)
+    g.tensor.wait_ge(T.sem["lds"], 16)
+    for k, (a, n, _v) in enumerate(pieces):
+        g.tensor.wait_ge(T.sem["ldc%d" % k], 16)
+        for b in range(4):
+            u = 4 * k + b
+            if k == 0:
+                g.tensor.wait_ge(T.sem["sel%d" % b], 1)
+            if u >= NBANK:
+                g.tensor.wait_ge(T.sem["ev%d_%d" % ((u - NBANK) // 4, b)], 1)
+            o = BANK * (u % NBANK)
+            g.tensor.matmul_mx(T.ps[:, o:o + n], T.sc[:, 128 * b:128 * b + 128], T.ss[:, 128 * b:128 * b + 128],
+                               T.kcb[:, a:a + n], T.ksb[:, a:a + n], True, True).then_inc(T.sem["mm%d_%d" % (k, b)], 1)
+    for k, (a, n, _v) in enumerate(pieces):
+        for b in range(4):
+            o = BANK * ((4 * k + b) % NBANK)
+            dst = T.t[:, 4 * a + b:4 * (a + n):4]
+            mm, ev = T.sem["mm%d_%d" % (k, b)], T.sem["ev%d_%d" % (k, b)]
+            if b % 2 == 0:
+                g.vector.wait_ge(mm, 1)
+                g.vector.tensor_scalar(dst, T.ps[:, o:o + n], SCALE, None, AluOpType.mult).then_inc(ev, 1)
+            else:
+                g.scalar.wait_ge(mm, 1)
+                g.scalar.activation(dst, T.ps[:, o:o + n], ActivationFunctionType.Copy, scale=SCALE).then_inc(ev, 1)
+        for b in range(4):
+            g.vector.wait_ge(T.sem["ev%d_%d" % (k, b)], 1)
+        g.vector.quantize_mx(T.nc[:, a:a + n], T.ns[:, a:a + n], T.t[:, 4 * a:4 * (a + n)]).then_inc(T.sem["new%d" % k], 1)
+    sent = 0
+    for k, (a, n, via) in enumerate(pieces):
+        g.wait_ge(T.sem["new%d" % k], 1)
+        dst = T.cores[own[r]] if via is None else via
+        sent += send(g, T, topo, core, dst, T.nc[:, a:a + n], T.ns[:, a:a + n], r, a, n, T.sem["arr%d_%d" % (r, k)])
+    return sent
+
+
+def consumer(g, core, T, topo, routes, own, r):
+    g.sync.dma_start(T.qb[:], T.q[:]).then_inc(T.sem["ldq"], 16)
+    g.scalar.dma_start(T.kcb[:].bitcast(dt.uint8), T.kc[:]).then_inc(T.sem["ldc0"], 16)
+    g.sync.dma_start(T.ksb[:], T.ks[:]).then_inc(T.sem["lds"], 16)
+    g.vector.wait_ge(T.sem["ldq"], 16)
+    g.vector.quantize_mx(T.qc[:], T.qs[:], T.qb[:]).then_inc(T.sem["qq"], 1)
+    mine = [p for p in range(NR) if p != r and own[p] == r]
+    col = {p: KT * (i + 1) for i, p in enumerate(mine)}
+    units = [(-1, 0, r, 0, KT)]
+    for p in mine:
+        for k, (a, n, via) in enumerate(routes[p]):
+            late = 0 if topo.chip(T.cores[p]) == topo.chip(core) else (1 if via is None else 2)
+            units.append((late, k, p, a, n))
+    units.sort()
+    last = len(units) - 1
+    nstore = [0, 0]
+    for u, (late, k, p, a, n) in enumerate(units):
+        if late < 0:
+            g.tensor.wait_ge(T.sem["qq"], 1)
+            g.tensor.wait_ge(T.sem["ldc0"], 16)
+            g.tensor.wait_ge(T.sem["lds"], 16)
+            codes, scales, out = T.kcb[:], T.ksb[:], 0
+        else:
+            via = routes[p][k][2]
+            _m, ne = engines(topo, T.cores[p] if via is None else via, core)
+            g.tensor.wait_ge(T.sem["arr%d_%d" % (p, k)], 2 * ne)
+            lo = p * KT + a
+            codes, scales, out = T.lc[:, lo:lo + n], T.ls[:, lo:lo + n], col[p] + a
+        if u >= NBANK:
+            g.tensor.wait_ge(T.sem["ue%d" % (u - NBANK)], 1)
+        o = BANK * (u % NBANK)
+        g.tensor.matmul_mx(T.ps[:, o:o + n], T.qc[:], T.qs[:], codes, scales, True, True).then_inc(T.sem["um%d" % u], 1)
+        ue = T.sem["ue%d" % u]
+        if (last - u) % 2 == 0:
+            g.scalar.wait_ge(T.sem["um%d" % u], 1)
+            g.scalar.activation(T.yb[:, out:out + n], T.ps[:, o:o + n], ActivationFunctionType.Copy).then_inc(ue, 1)
+        else:
+            g.vector.wait_ge(T.sem["um%d" % u], 1)
+            g.vector.tensor_copy(T.yb[:, out:out + n], T.ps[:, o:o + n]).then_inc(ue, 1)
+        q, sem, i = (g.scalar, "store2", 1) if u == last else (g.sync, "store", 0)
+        q.wait_ge(ue, 1)
+        q.dma_start(T.y[:, out:out + n], T.yb[:, out:out + n]).then_inc(T.sem[sem], 16)
+        nstore[i] += 16
+    g.sync.wait_ge(T.sem["store"], nstore[0])
+    g.scalar.wait_ge(T.sem["store2"], nstore[1])
+
+
+def rank_program(g, core, T, topo):
+    own = T.tables["OWN"]
+    routes = plan(T, topo)
+    r = T.rank_of(core)
+    sent = 0
+    if r is not None:
+        if own[r] == r:
+            consumer(g, core, T, topo, routes, own, r)
+        else:
+            sent += producer(g, core, T, topo, routes, own, r)
+    sent += forward(g, core, T, topo, routes, own)
+    if sent:
+        g.wait_ge(T.sem["sent"], sent)

@@ -4,8 +4,10 @@ KT = 384
 NR = 8
 BANK = 512
 NBANK = 8
-MAXP = 3
 SCALE = 0.8
+SPLIT = {0: [192, 192], 1: [192, 192], 2: [192, 192]}
+WHOLE = [0]
+MAXP = 3
 
 SCRATCH = {
     "kcb": ("sbuf", [128, KT], "float8_e4m3fn_x4"),
@@ -30,7 +32,8 @@ SEMAPHORES = (["ldq", "lds", "zero", "one", "qq", "sent", "store", "store2"]
               + ["mm%d_%d" % (k, b) for k in range(MAXP) for b in range(4)]
               + ["ev%d_%d" % (k, b) for k in range(MAXP) for b in range(4)]
               + ["new%d" % k for k in range(MAXP)]
-              + ["arr%d_%d" % (r, k) for r in range(NR) for k in range(MAXP)]
+              + ["arc%d_%d" % (r, k) for r in range(NR) for k in range(MAXP)]
+              + ["ars%d_%d" % (r, k) for r in range(NR) for k in range(MAXP)]
               + ["um%d" % u for u in range(NR * MAXP)]
               + ["ue%d" % u for u in range(NR * MAXP)])
 
@@ -51,41 +54,52 @@ def plan(T, topo):
         if own[r] == r:
             continue
         dst = T.cores[own[r]]
+        via = None
         if topo.may_write(c, dst):
-            cols, via = [(0, KT)], None
+            kind = 0 if topo.chip(c) == topo.chip(dst) else 1
         else:
+            kind = 2
             idle = [x for x in range(8 * topo.chip(c), 8 * topo.chip(c) + 8)
                     if x not in T.cores and topo.chip(x) == topo.chip(c) and topo.may_write(x, dst)]
             via = idle[blocked % len(idle)]
             blocked += 1
-            cols = [(0, KT // 2), (KT // 2, KT // 2)]
-        out[r] = [(a, n, via) for a, n in cols]
+        out[r] = (kind, [(sum(SPLIT[kind][:i]), n, via) for i, n in enumerate(SPLIT[kind])])
     return out
 
 
-def send(g, T, topo, src, dst, codes, scales, r, a, n, sem):
+def send_scales(g, T, topo, src, dst, scales, r, a, n, k):
     mask, ne = engines(topo, src, dst)
     rid, pid, _s = topo.addr(dst)
     lo = r * KT + a
-    g.remote_dma(T.lc[:, lo:lo + n].bitcast(dt.uint8), codes.bitcast(dt.uint8), sem, T.sem["sent"], pid, rid, mask)
-    g.remote_dma(T.ls[:, lo:lo + n], scales, sem, T.sem["sent"], pid, rid, mask)
-    return 2 * ne
+    g.remote_dma(T.ls[:, lo:lo + n], scales, T.sem["ars%d_%d" % (r, k)], T.sem["sent"], pid, rid, mask)
+    return ne
+
+
+def send_codes(g, T, topo, src, dst, codes, r, a, n, k):
+    mask, ne = engines(topo, src, dst)
+    rid, pid, _s = topo.addr(dst)
+    lo = r * KT + a
+    g.remote_dma(T.lc[:, lo:lo + n].bitcast(dt.uint8), codes.bitcast(dt.uint8), T.sem["arc%d_%d" % (r, k)],
+                 T.sem["sent"], pid, rid, mask)
+    return ne
 
 
 def forward(g, core, T, topo, routes, own):
     sent = 0
-    todo = [(k, r, p) for r in routes for k, p in enumerate(routes[r]) if p[2] == core]
+    todo = [(k, r, p) for r in routes for k, p in enumerate(routes[r][1]) if p[2] == core]
     for k, r, (a, n, _via) in sorted(todo):
         _m, ne = engines(topo, T.cores[r], core)
-        sem = T.sem["arr%d_%d" % (r, k)]
         lo = r * KT + a
-        g.wait_ge(sem, 2 * ne)
-        sent += send(g, T, topo, core, T.cores[own[r]], T.lc[:, lo:lo + n], T.ls[:, lo:lo + n], r, a, n, sem)
+        dst = T.cores[own[r]]
+        g.wait_ge(T.sem["ars%d_%d" % (r, k)], ne)
+        sent += send_scales(g, T, topo, core, dst, T.ls[:, lo:lo + n], r, a, n, k)
+        g.wait_ge(T.sem["arc%d_%d" % (r, k)], ne)
+        sent += send_codes(g, T, topo, core, dst, T.lc[:, lo:lo + n], r, a, n, k)
     return sent
 
 
 def producer(g, core, T, topo, routes, own, r):
-    pieces = routes[r]
+    pieces = routes[r][1]
     for k, (a, n, _v) in enumerate(pieces):
         g.sync.dma_start(T.kcb[:, a:a + n].bitcast(dt.uint8), T.kc[:, 4 * a:4 * (a + n)]).then_inc(T.sem["ldc%d" % k], 16)
     g.scalar.dma_start(T.ksb[:], T.ks[:]).then_inc(T.sem["lds"], 16)
@@ -126,7 +140,8 @@ def producer(g, core, T, topo, routes, own, r):
     for k, (a, n, via) in enumerate(pieces):
         g.wait_ge(T.sem["new%d" % k], 1)
         dst = T.cores[own[r]] if via is None else via
-        sent += send(g, T, topo, core, dst, T.nc[:, a:a + n], T.ns[:, a:a + n], r, a, n, T.sem["arr%d_%d" % (r, k)])
+        sent += send_scales(g, T, topo, core, dst, T.ns[:, a:a + n], r, a, n, k)
+        sent += send_codes(g, T, topo, core, dst, T.nc[:, a:a + n], r, a, n, k)
     return sent
 
 
@@ -138,24 +153,21 @@ def consumer(g, core, T, topo, routes, own, r):
     g.vector.quantize_mx(T.qc[:], T.qs[:], T.qb[:]).then_inc(T.sem["qq"], 1)
     mine = [p for p in range(NR) if p != r and own[p] == r]
     col = {p: KT * (i + 1) for i, p in enumerate(mine)}
-    units = [(-1, 0, r, 0, KT)]
-    for p in mine:
-        for k, (a, n, via) in enumerate(routes[p]):
-            late = 0 if topo.chip(T.cores[p]) == topo.chip(core) else (1 if via is None else 2)
-            units.append((late, k, p, a, n))
-    units.sort()
+    units = sorted([(-1, 0, r, 0, KT)] + [(routes[p][0], k, p, a, n) for p in mine
+                                          for k, (a, n, _v) in enumerate(routes[p][1])])
     last = len(units) - 1
     nstore = [0, 0]
-    for u, (late, k, p, a, n) in enumerate(units):
-        if late < 0:
+    for u, (kind, k, p, a, n) in enumerate(units):
+        if kind < 0:
             g.tensor.wait_ge(T.sem["qq"], 1)
             g.tensor.wait_ge(T.sem["ldc0"], 16)
             g.tensor.wait_ge(T.sem["lds"], 16)
             codes, scales, out = T.kcb[:], T.ksb[:], 0
         else:
-            via = routes[p][k][2]
+            via = routes[p][1][k][2]
             _m, ne = engines(topo, T.cores[p] if via is None else via, core)
-            g.tensor.wait_ge(T.sem["arr%d_%d" % (p, k)], 2 * ne)
+            g.tensor.wait_ge(T.sem["ars%d_%d" % (p, k)], ne)
+            g.tensor.wait_ge(T.sem["arc%d_%d" % (p, k)], ne)
             lo = p * KT + a
             codes, scales, out = T.lc[:, lo:lo + n], T.ls[:, lo:lo + n], col[p] + a
         if u >= NBANK:
@@ -171,7 +183,12 @@ def consumer(g, core, T, topo, routes, own, r):
             g.vector.tensor_copy(T.yb[:, out:out + n], T.ps[:, o:o + n]).then_inc(ue, 1)
         q, sem, i = (g.scalar, "store2", 1) if u == last else (g.sync, "store", 0)
         q.wait_ge(ue, 1)
-        q.dma_start(T.y[:, out:out + n], T.yb[:, out:out + n]).then_inc(T.sem[sem], 16)
+        lo, hi = out, out + n
+        if kind in WHOLE:
+            if a + n < KT:
+                continue
+            lo = col[p]
+        q.dma_start(T.y[:, lo:hi], T.yb[:, lo:hi]).then_inc(T.sem[sem], 16)
         nstore[i] += 16
     g.sync.wait_ge(T.sem["store"], nstore[0])
     g.scalar.wait_ge(T.sem["store2"], nstore[1])

@@ -5,8 +5,9 @@ NR = 8
 BANK = 512
 NBANK = 8
 SCALE = 0.8
-SPLIT = {0: [192, 192], 1: [192, 192], 2: [192, 192]}
-WHOLE = [0]
+SPLIT = {0: [128, 256], 1: [128, 256], 2: [128, 128, 128]}
+BY_RANK = [2]
+STORE = {-1: {0: 0}, 0: {1: 0}, 1: {1: 0}, 2: {1: 0, 2: 2}}
 MAXP = 3
 
 SCRATCH = {
@@ -26,7 +27,7 @@ SCRATCH = {
     "yb": ("sbuf", [128, NR * KT], "float32"),
     "ps": ("psum", [128, BANK * NBANK], "float32"),
 }
-SEMAPHORES = (["ldq", "lds", "zero", "one", "qq", "sent", "store", "store2"]
+SEMAPHORES = (["ldq", "lds", "zero", "zero2", "one", "qq", "sent", "store", "store2"]
               + ["ldc%d" % k for k in range(MAXP)]
               + ["sel%d" % b for b in range(4)]
               + ["mm%d_%d" % (k, b) for k in range(MAXP) for b in range(4)]
@@ -54,16 +55,18 @@ def plan(T, topo):
         if own[r] == r:
             continue
         dst = T.cores[own[r]]
-        via = None
+        vias = [None] * MAXP
         if topo.may_write(c, dst):
             kind = 0 if topo.chip(c) == topo.chip(dst) else 1
         else:
             kind = 2
-            idle = [x for x in range(8 * topo.chip(c), 8 * topo.chip(c) + 8)
-                    if x not in T.cores and topo.chip(x) == topo.chip(c) and topo.may_write(x, dst)]
-            via = idle[blocked % len(idle)]
+            able = [x for x in range(8 * topo.chip(c), 8 * topo.chip(c) + 8)
+                    if x != c and topo.chip(x) == topo.chip(c) and topo.may_write(x, dst)]
+            idle = [x for x in able if x not in T.cores]
+            busy = [x for x in able if x in T.cores]
+            vias = [busy[blocked % len(busy)] if k in BY_RANK else idle[blocked % len(idle)] for k in range(MAXP)]
             blocked += 1
-        out[r] = (kind, [(sum(SPLIT[kind][:i]), n, via) for i, n in enumerate(SPLIT[kind])])
+        out[r] = (kind, [(sum(SPLIT[kind][:i]), n, vias[i]) for i, n in enumerate(SPLIT[kind])])
     return out
 
 
@@ -103,9 +106,12 @@ def producer(g, core, T, topo, routes, own, r):
     for k, (a, n, _v) in enumerate(pieces):
         g.sync.dma_start(T.kcb[:, a:a + n].bitcast(dt.uint8), T.kc[:, 4 * a:4 * (a + n)]).then_inc(T.sem["ldc%d" % k], 16)
     g.scalar.dma_start(T.ksb[:], T.ks[:]).then_inc(T.sem["lds"], 16)
-    g.vector.memset(T.z[:], 0.0).then_inc(T.sem["zero"], 1)
+    g.vector.memset(T.z[:, 3:515:4], 0.0).then_inc(T.sem["zero"], 1)
+    for t in range(3):
+        g.vector.memset(T.z[:, t:513 + t:4], 0.0).then_inc(T.sem["zero2"], 1)
     g.wait_ge(T.sem["zero"], 1)
     g.affine_select(T.z[:, 3:515:4], T.z[:, 3:515:4], [[-1, 128]], AluOpType.not_equal, 1.0, 0, 1).then_inc(T.sem["one"], 1)
+    g.vector.wait_ge(T.sem["zero2"], 3)
     g.vector.wait_ge(T.sem["one"], 1)
     for b in range(4):
         g.vector.quantize_mx(T.sc[:, 128 * b:128 * b + 128], T.ss[:, 128 * b:128 * b + 128],
@@ -153,6 +159,7 @@ def consumer(g, core, T, topo, routes, own, r):
     g.vector.quantize_mx(T.qc[:], T.qs[:], T.qb[:]).then_inc(T.sem["qq"], 1)
     mine = [p for p in range(NR) if p != r and own[p] == r]
     col = {p: KT * (i + 1) for i, p in enumerate(mine)}
+    col[r] = 0
     units = sorted([(-1, 0, r, 0, KT)] + [(routes[p][0], k, p, a, n) for p in mine
                                           for k, (a, n, _v) in enumerate(routes[p][1])])
     last = len(units) - 1
@@ -162,14 +169,15 @@ def consumer(g, core, T, topo, routes, own, r):
             g.tensor.wait_ge(T.sem["qq"], 1)
             g.tensor.wait_ge(T.sem["ldc0"], 16)
             g.tensor.wait_ge(T.sem["lds"], 16)
-            codes, scales, out = T.kcb[:], T.ksb[:], 0
+            codes, scales = T.kcb[:], T.ksb[:]
         else:
             via = routes[p][1][k][2]
             _m, ne = engines(topo, T.cores[p] if via is None else via, core)
             g.tensor.wait_ge(T.sem["ars%d_%d" % (p, k)], ne)
             g.tensor.wait_ge(T.sem["arc%d_%d" % (p, k)], ne)
             lo = p * KT + a
-            codes, scales, out = T.lc[:, lo:lo + n], T.ls[:, lo:lo + n], col[p] + a
+            codes, scales = T.lc[:, lo:lo + n], T.ls[:, lo:lo + n]
+        out = col[p] + a
         if u >= NBANK:
             g.tensor.wait_ge(T.sem["ue%d" % (u - NBANK)], 1)
         o = BANK * (u % NBANK)
@@ -183,13 +191,11 @@ def consumer(g, core, T, topo, routes, own, r):
             g.vector.tensor_copy(T.yb[:, out:out + n], T.ps[:, o:o + n]).then_inc(ue, 1)
         q, sem, i = (g.scalar, "store2", 1) if u == last else (g.sync, "store", 0)
         q.wait_ge(ue, 1)
-        lo, hi = out, out + n
-        if kind in WHOLE:
-            if a + n < KT:
-                continue
-            lo = col[p]
-        q.dma_start(T.y[:, lo:hi], T.yb[:, lo:hi]).then_inc(T.sem[sem], 16)
-        nstore[i] += 16
+        if k in STORE[kind]:
+            first = STORE[kind][k]
+            lo = out if first == k else col[p] + routes[p][1][first][0]
+            q.dma_start(T.y[:, lo:out + n], T.yb[:, lo:out + n]).then_inc(T.sem[sem], 16)
+            nstore[i] += 16
     g.sync.wait_ge(T.sem["store"], nstore[0])
     g.scalar.wait_ge(T.sem["store2"], nstore[1])
 

from concourse.mybir import dt, AluOpType, ActivationFunctionType

KT = 384
NR = 8
BANK = 512
NBANK = 8
SCALE = 0.8
SPLIT = {0: [128, 256], 1: [128, 256], 2: [128, 128, 128]}
BY_RANK = [2]
STORE = {-1: {0: 0}, 0: {1: 0}, 1: {1: 0}, 2: {1: 0, 2: 2}}
MAXP = 3

SCRATCH = {
    "kcb": ("sbuf", [128, KT], "float8_e4m3fn_x4"),
    "ksb": ("sbuf", [128, KT], "uint8"),
    "z": ("sbuf", [128, 516], "bfloat16"),
    "sc": ("sbuf", [128, 512], "float8_e4m3fn_x4"),
    "ss": ("sbuf", [128, 512], "uint8"),
    "t": ("sbuf", [128, 4 * KT], "bfloat16"),
    "nc": ("sbuf", [128, KT], "float8_e4m3fn_x4"),
    "ns": ("sbuf", [128, KT], "uint8"),
    "qb": ("sbuf", [128, 512], "bfloat16"),
    "qc": ("sbuf", [128, 128], "float8_e4m3fn_x4"),
    "qs": ("sbuf", [128, 128], "uint8"),
    "lc": ("sbuf", [128, NR * KT], "float8_e4m3fn_x4"),
    "ls": ("sbuf", [128, NR * KT], "uint8"),
    "yb": ("sbuf", [128, NR * KT], "float32"),
    "ps": ("psum", [128, BANK * NBANK], "float32"),
}
SEMAPHORES = (["ldq", "lds", "zero", "zero2", "one", "qq", "sent", "store", "store2"]
              + ["ldc%d" % k for k in range(MAXP)]
              + ["sel%d" % b for b in range(4)]
              + ["mm%d_%d" % (k, b) for k in range(MAXP) for b in range(4)]
              + ["ev%d_%d" % (k, b) for k in range(MAXP) for b in range(4)]
              + ["new%d" % k for k in range(MAXP)]
              + ["arc%d_%d" % (r, k) for r in range(NR) for k in range(MAXP)]
              + ["ars%d_%d" % (r, k) for r in range(NR) for k in range(MAXP)]
              + ["um%d" % u for u in range(NR * MAXP)]
              + ["ue%d" % u for u in range(NR * MAXP)])


def engines(topo, src, dst):
    m = topo.mask(src, dst)
    bits = [i for i in range(m.bit_length()) if (m >> i) & 1]
    if topo.chip(src) == topo.chip(dst):
        bits = bits[::2]
    return sum(1 << i for i in bits), len(bits)


def plan(T, topo):
    own = T.tables["OWN"]
    out = {}
    blocked = 0
    for r, c in enumerate(T.cores):
        if own[r] == r:
            continue
        dst = T.cores[own[r]]
        vias = [None] * MAXP
        if topo.may_write(c, dst):
            kind = 0 if topo.chip(c) == topo.chip(dst) else 1
        else:
            kind = 2
            able = [x for x in range(8 * topo.chip(c), 8 * topo.chip(c) + 8)
                    if x != c and topo.chip(x) == topo.chip(c) and topo.may_write(x, dst)]
            idle = [x for x in able if x not in T.cores]
            busy = [x for x in able if x in T.cores]
            vias = [busy[blocked % len(busy)] if k in BY_RANK else idle[blocked % len(idle)] for k in range(MAXP)]
            blocked += 1
        out[r] = (kind, [(sum(SPLIT[kind][:i]), n, vias[i]) for i, n in enumerate(SPLIT[kind])])
    return out


def send_scales(g, T, topo, src, dst, scales, r, a, n, k):
    mask, ne = engines(topo, src, dst)
    rid, pid, _s = topo.addr(dst)
    lo = r * KT + a
    g.remote_dma(T.ls[:, lo:lo + n], scales, T.sem["ars%d_%d" % (r, k)], T.sem["sent"], pid, rid, mask)
    return ne


def send_codes(g, T, topo, src, dst, codes, r, a, n, k):
    mask, ne = engines(topo, src, dst)
    rid, pid, _s = topo.addr(dst)
    lo = r * KT + a
    g.remote_dma(T.lc[:, lo:lo + n].bitcast(dt.uint8), codes.bitcast(dt.uint8), T.sem["arc%d_%d" % (r, k)],
                 T.sem["sent"], pid, rid, mask)
    return ne


def forward(g, core, T, topo, routes, own):
    sent = 0
    todo = [(k, r, p) for r in routes for k, p in enumerate(routes[r][1]) if p[2] == core]
    for k, r, (a, n, _via) in sorted(todo):
        _m, ne = engines(topo, T.cores[r], core)
        lo = r * KT + a
        dst = T.cores[own[r]]
        g.wait_ge(T.sem["ars%d_%d" % (r, k)], ne)
        sent += send_scales(g, T, topo, core, dst, T.ls[:, lo:lo + n], r, a, n, k)
        g.wait_ge(T.sem["arc%d_%d" % (r, k)], ne)
        sent += send_codes(g, T, topo, core, dst, T.lc[:, lo:lo + n], r, a, n, k)
    return sent


def producer(g, core, T, topo, routes, own, r):
    pieces = routes[r][1]
    for k, (a, n, _v) in enumerate(pieces):
        g.sync.dma_start(T.kcb[:, a:a + n].bitcast(dt.uint8), T.kc[:, 4 * a:4 * (a + n)]).then_inc(T.sem["ldc%d" % k], 16)
    g.scalar.dma_start(T.ksb[:], T.ks[:]).then_inc(T.sem["lds"], 16)
    g.vector.memset(T.z[:, 3:515:4], 0.0).then_inc(T.sem["zero"], 1)
    for t in range(3):
        g.vector.memset(T.z[:, t:513 + t:4], 0.0).then_inc(T.sem["zero2"], 1)
    g.wait_ge(T.sem["zero"], 1)
    g.affine_select(T.z[:, 3:515:4], T.z[:, 3:515:4], [[-1, 128]], AluOpType.not_equal, 1.0, 0, 1).then_inc(T.sem["one"], 1)
    g.vector.wait_ge(T.sem["zero2"], 3)
    g.vector.wait_ge(T.sem["one"], 1)
    for b in range(4):
        g.vector.quantize_mx(T.sc[:, 128 * b:128 * b + 128], T.ss[:, 128 * b:128 * b + 128],
                             T.z[:, 3 - b:515 - b]).then_inc(T.sem["sel%d" % b], 1)
    g.tensor.wait_ge(T.sem["lds"], 16)
    for k, (a, n, _v) in enumerate(pieces):
        g.tensor.wait_ge(T.sem["ldc%d" % k], 16)
        for b in range(4):
            u = 4 * k + b
            if k == 0:
                g.tensor.wait_ge(T.sem["sel%d" % b], 1)
            if u >= NBANK:
                g.tensor.wait_ge(T.sem["ev%d_%d" % ((u - NBANK) // 4, b)], 1)
            o = BANK * (u % NBANK)
            g.tensor.matmul_mx(T.ps[:, o:o + n], T.sc[:, 128 * b:128 * b + 128], T.ss[:, 128 * b:128 * b + 128],
                               T.kcb[:, a:a + n], T.ksb[:, a:a + n], True, True).then_inc(T.sem["mm%d_%d" % (k, b)], 1)
    for k, (a, n, _v) in enumerate(pieces):
        for b in range(4):
            o = BANK * ((4 * k + b) % NBANK)
            dst = T.t[:, 4 * a + b:4 * (a + n):4]
            mm, ev = T.sem["mm%d_%d" % (k, b)], T.sem["ev%d_%d" % (k, b)]
            if b % 2 == 0:
                g.vector.wait_ge(mm, 1)
                g.vector.tensor_scalar(dst, T.ps[:, o:o + n], SCALE, None, AluOpType.mult).then_inc(ev, 1)
            else:
                g.scalar.wait_ge(mm, 1)
                g.scalar.activation(dst, T.ps[:, o:o + n], ActivationFunctionType.Copy, scale=SCALE).then_inc(ev, 1)
        for b in range(4):
            g.vector.wait_ge(T.sem["ev%d_%d" % (k, b)], 1)
        g.vector.quantize_mx(T.nc[:, a:a + n], T.ns[:, a:a + n], T.t[:, 4 * a:4 * (a + n)]).then_inc(T.sem["new%d" % k], 1)
    sent = 0
    for k, (a, n, via) in enumerate(pieces):
        g.wait_ge(T.sem["new%d" % k], 1)
        dst = T.cores[own[r]] if via is None else via
        sent += send_scales(g, T, topo, core, dst, T.ns[:, a:a + n], r, a, n, k)
        sent += send_codes(g, T, topo, core, dst, T.nc[:, a:a + n], r, a, n, k)
    return sent


def consumer(g, core, T, topo, routes, own, r):
    g.sync.dma_start(T.qb[:], T.q[:]).then_inc(T.sem["ldq"], 16)
    g.scalar.dma_start(T.kcb[:].bitcast(dt.uint8), T.kc[:]).then_inc(T.sem["ldc0"], 16)
    g.sync.dma_start(T.ksb[:], T.ks[:]).then_inc(T.sem["lds"], 16)
    g.vector.wait_ge(T.sem["ldq"], 16)
    g.vector.quantize_mx(T.qc[:], T.qs[:], T.qb[:]).then_inc(T.sem["qq"], 1)
    mine = [p for p in range(NR) if p != r and own[p] == r]
    col = {p: KT * (i + 1) for i, p in enumerate(mine)}
    col[r] = 0
    units = sorted([(-1, 0, r, 0, KT)] + [(routes[p][0], k, p, a, n) for p in mine
                                          for k, (a, n, _v) in enumerate(routes[p][1])])
    last = len(units) - 1
    nstore = [0, 0]
    for u, (kind, k, p, a, n) in enumerate(units):
        if kind < 0:
            g.tensor.wait_ge(T.sem["qq"], 1)
            g.tensor.wait_ge(T.sem["ldc0"], 16)
            g.tensor.wait_ge(T.sem["lds"], 16)
            codes, scales = T.kcb[:], T.ksb[:]
        else:
            via = routes[p][1][k][2]
            _m, ne = engines(topo, T.cores[p] if via is None else via, core)
            g.tensor.wait_ge(T.sem["ars%d_%d" % (p, k)], ne)
            g.tensor.wait_ge(T.sem["arc%d_%d" % (p, k)], ne)
            lo = p * KT + a
            codes, scales = T.lc[:, lo:lo + n], T.ls[:, lo:lo + n]
        out = col[p] + a
        if u >= NBANK:
            g.tensor.wait_ge(T.sem["ue%d" % (u - NBANK)], 1)
        o = BANK * (u % NBANK)
        g.tensor.matmul_mx(T.ps[:, o:o + n], T.qc[:], T.qs[:], codes, scales, True, True).then_inc(T.sem["um%d" % u], 1)
        ue = T.sem["ue%d" % u]
        if (last - u) % 2 == 0:
            g.scalar.wait_ge(T.sem["um%d" % u], 1)
            g.scalar.activation(T.yb[:, out:out + n], T.ps[:, o:o + n], ActivationFunctionType.Copy).then_inc(ue, 1)
        else:
            g.vector.wait_ge(T.sem["um%d" % u], 1)
            g.vector.tensor_copy(T.yb[:, out:out + n], T.ps[:, o:o + n]).then_inc(ue, 1)
        q, sem, i = (g.scalar, "store2", 1) if u == last else (g.sync, "store", 0)
        q.wait_ge(ue, 1)
        if k in STORE[kind]:
            first = STORE[kind][k]
            lo = out if first == k else col[p] + routes[p][1][first][0]
            q.dma_start(T.y[:, lo:out + n], T.yb[:, lo:out + n]).then_inc(T.sem[sem], 16)
            nstore[i] += 16
    g.sync.wait_ge(T.sem["store"], nstore[0])
    g.scalar.wait_ge(T.sem["store2"], nstore[1])


def rank_program(g, core, T, topo):
    own = T.tables["OWN"]
    routes = plan(T, topo)
    r = T.rank_of(core)
    sent = 0
    if r is not None:
        if own[r] == r:
            consumer(g, core, T, topo, routes, own, r)
        else:
            sent += producer(g, core, T, topo, routes, own, r)
    sent += forward(g, core, T, topo, routes, own)
    if sent:
        g.wait_ge(T.sem["sent"], sent)
